import numpy as np
CORES = [0,1,2,3,4,5,6,7,8,9,10,11,12,13,14,15]
N = 16
def setup_inputs(rng):
    return {"x1": rng.standard_normal((N, 128, 256), dtype=np.float32), "x2": rng.standard_normal((N, 128, 1024), dtype=np.float32)}
def reference(x1, x2):
    out = []
    s = x1.sum(axis=0, dtype=np.float64).astype(x1.dtype)
    b = 256 // N
    out.append(np.stack([s[:, r * b:(r + 1) * b] for r in range(N)]))
    out.append(np.broadcast_to(x2[11], x2.shape))
    return {"y1": out[0], "y2": out[1]}

@@ -1,0 +1,271 @@
+from concourse.bass import DstId, RemoteDMATransfer
+from concourse.mybir import AluOpType
+
+K = 2
+RS = 2
+SP3 = "ten"
+ORDER = "AABB"
+FUSE = True
+
+ROOT = 11
+W = 128 // K
+SCRATCH = {
+    "xs": ("sbuf", [128, 256], "float32"),
+    "rl": ("sbuf", [128, 1024 if RS == 2 else 256], "float32"),
+    "p0": ("dram", [128, 16], "float32"),
+    "p1": ("dram", [128, 16], "float32"),
+    "bb": ("dram", [8 * K, 128, W], "float32"),
+}
+SEMAPHORES = ["ld1", "y1a", "y1b", "snt", "rsA", "rs0", "rs1"] + [
+    n + r for n in ("ld2", "y2", "bcS", "bcX", "bcG", "bcH") for r in "abcd"]
+
+CARRIER = (ROOT, ROOT, 10, 10, 14, 14, 15, 15)
+SPREADER = (8, 9, 10, 10, 14, 12, 15, 13)
+ALL = (slice(None),)
+
+
+def eng(lo, n):
+    return ((1 << n) - 1) << lo
+
+
+def cols(a, n):
+    return (slice(None), slice(a, a + n))
+
+
+def piece(t, j):
+    return ("bb", (8 * t + j,))
+
+
+def part(name, t):
+    if name == "bb":
+        return (name, (slice(8 * t, 8 * t + 8),))
+    return (name, (slice(t * 128 // K, (t + 1) * 128 // K), slice(None)))
+
+
+def after(c, cores):
+    return sorted(cores, key=lambda d: (d - c) % 8)
+
+
+def groups(ch):
+    if RS == 2:
+        return [((3, 15)[ch], 0, list(range(4, 12))), ((7, 10)[ch], 128, [12, 13, 14, 15, 0, 1, 2, 3])]
+    out = []
+    for p in range(8):
+        red = 8 * ch + ((4, 0, 1, 5)[p % 4] if p // 4 == ch else (2, 3, 6, 7)[p % 4])
+        out.append((red, 32 * p, [2 * p, 2 * p + 1]))
+    return out
+
+
+def rs_load(c):
+    if RS == 2:
+        return [(("xs", cols(0, 192)), ("x1", cols(64, 192))), (("xs", cols(192, 64)), ("x1", cols(0, 64)))]
+    return [(("xs", ALL), ("x1", ALL))]
+
+
+def rs_send(c):
+    ch, k = divmod(c, 8)
+    gs = [x for x in groups(ch) if x[0] != c]
+    n = 8 if RS == 2 else 2
+    return [([("xs", cols(a, 16 * len(rk)))], [(red, ("rl", cols(16 * len(rk) * k, 16 * len(rk))))], eng(n * i, n),
+             "rsA", 0) for i, (red, a, rk) in enumerate(gs)]
+
+
+def rs_fold(c):
+    ch, k = divmod(c, 8)
+    trs = []
+    for red, a, rk in groups(ch):
+        if red != c:
+            continue
+        w = 16 * len(rk)
+        far = [r for r in rk if r // 8 != ch]
+        near = [r for r in rk if r // 8 == ch]
+        nf = 8 // len(far) if far else 0
+        nn = (8 if far else 16) // len(near) if near else 0
+        for r in rk:
+            o = 16 * rk.index(r)
+            srcs = [("rl", cols(w * s + o, 16)) for s in range(8) if s != k] + [("xs", cols(a + o, 16))]
+            m = eng(nf * far.index(r), nf) if r in far else eng((8 if far else 0) + nn * near.index(r), nn)
+            trs.append((srcs, [(r, ("p%d" % ch, ALL))], m, "rs%d" % ch, 1))
+    return trs
+
+
+def spread(t, j, c, mask, dests=None, sem="bcG"):
+    if dests is None:
+        have = (ROOT, CARRIER[j], SPREADER[j])
+        dests = [d for d in range(8, 16) if d not in have]
+    return ([piece(t, j)], [(d, piece(t, j)) for d in after(c, dests)], mask, sem + "abcd"[t], 0)
+
+
+def prog(c):
+    ch, k = divmod(c, 8)
+    ops = []
+    rounds = range(K)
+    folds = rs_fold(c)
+
+    def dma(out, in_, sem, add=False):
+        ops.append(("dma", out, in_, sem, add))
+
+    def wait(*sems):
+        for s in sems:
+            ops.append(("wait", s))
+
+    def call(trs):
+        ops.append(("rdma", trs))
+
+    def load_x1():
+        for o, i in rs_load(c):
+            dma(o, i, "ld1")
+
+    def send_x1():
+        wait("ld1")
+        call(rs_send(c))
+
+    def fold_x1():
+        if folds:
+            wait("rsA")
+            call(folds)
+
+    if c == ROOT:
+        for t in rounds:
+            dma(part("bb", t), part("x2", t), "ld2" + "abcd"[t])
+        load_x1()
+
+        def call_a(t):
+            wait("ld2" + "abcd"[t])
+            call([([piece(t, j)], [(j if CARRIER[j] == ROOT else CARRIER[j], piece(t, j))], eng(2 * j, 2),
+                   ("bcX" if CARRIER[j] == ROOT else "bcS") + "abcd"[t], 0) for j in range(8)])
+
+        def call_b(t):
+            extra = [j for j in range(8) if SPREADER[j] != CARRIER[j]]
+            n = 4 if len(extra) <= 4 else 2
+            call([([piece(t, j)], [(SPREADER[j], piece(t, j))], eng(n * i, n), "bcS" + "abcd"[t], 0)
+                  for i, j in enumerate(extra)])
+
+        def call_s(t):
+            if SP3 == "root":
+                call([spread(t, 3, c, 0xFFFF)])
+
+        if ORDER == "ABAB":
+            for t in rounds:
+                call_a(t)
+                call_b(t)
+                call_s(t)
+        else:
+            for t in rounds:
+                call_a(t)
+            for t in rounds:
+                call_b(t)
+            for t in rounds:
+                call_s(t)
+        send_x1()
+        fold_x1()
+        dma(("y2", ALL), ("x2", ALL), "y2a")
+        wait("rs0")
+        dma(("y1", ALL), ("p0", ALL), "y1a")
+        wait("rs1", "y1a")
+        dma(("y1", ALL), ("p1", ALL), "y1b", True)
+        return ops
+
+    load_x1()
+    send_x1()
+    if ch == 0:
+        fold_x1()
+    for t in rounds:
+        if ch == 0:
+            wait("bcX" + "abcd"[t])
+            call([([piece(t, k)], [(d, piece(t, k)) for d in after(c, [d for d in range(8) if d != c])], 0xFFFF,
+                   "bcG" + "abcd"[t], 0)])
+        else:
+            wait("bcS" + "abcd"[t])
+            carry = [j for j in range(8) if CARRIER[j] == c]
+            own = [j for j in range(8) if SPREADER[j] == c]
+            if carry:
+                over = [([piece(t, j)], [(j, piece(t, j))], eng(4 * i, 4), "bcX" + "abcd"[t], 0)
+                        for i, j in enumerate(carry)]
+                if FUSE:
+                    call(over + [spread(t, own[0], c, eng(8, 8))])
+                    own = own[1:]
+                else:
+                    call(over)
+            for j in own:
+                if j == 3 and SP3 == "root":
+                    continue
+                if j == 3 and SP3 == "two":
+                    call([spread(t, j, c, 0xFFFF, [12, 13], "bcH")])
+                else:
+                    call([spread(t, j, c, 0xFFFF)])
+    if SP3 == "two" and c in (12, 13):
+        for t in rounds:
+            wait("bcH" + "abcd"[t])
+            call([spread(t, 3, c, 0xFFFF, [8, 14] if c == 12 else [9, 15])])
+    wait("rs0")
+    dma(("y1", ALL), ("p0", ALL), "y1a")
+    if ch == 1:
+        fold_x1()
+    for t in rounds:
+        wait("bcG" + "abcd"[t])
+        dma(part("y2", t), part("bb", t), "y2" + "abcd"[t])
+    wait("rs1", "y1a")
+    dma(("y1", ALL), ("p1", ALL), "y1b", True)
+    return ops
+
+
+def totals():
+    tot = {}
+
+    def add(c, s, n):
+        tot[(c, s)] = tot.get((c, s), 0) + n
+
+    for c in range(16):
+        for op in prog(c):
+            if op[0] == "dma":
+                add(c, op[3], 16)
+            elif op[0] == "rdma":
+                for srcs, dsts, mask, sem, alu in op[1]:
+                    n = bin(mask).count("1")
+                    add(c, "snt", n)
+                    for d, spec in dsts:
+                        add(d, sem, n)
+    return tot
+
+
+def rank_program(g, core, T, topo):
+    bufs = {"xs": T.xs, "rl": T.rl, "p0": T.p0, "p1": T.p1, "bb": T.bb,
+            "x1": T.x1, "x2": T.x2, "y1": T.y1, "y2": T.y2}
+    s = T.sem
+    sems = {"ld1": s.ld1, "y1a": s.y1a, "y1b": s.y1b, "snt": s.snt, "rsA": s.rsA, "rs0": s.rs0, "rs1": s.rs1,
+            "ld2a": s.ld2a, "ld2b": s.ld2b, "ld2c": s.ld2c, "ld2d": s.ld2d,
+            "y2a": s.y2a, "y2b": s.y2b, "y2c": s.y2c, "y2d": s.y2d,
+            "bcSa": s.bcSa, "bcSb": s.bcSb, "bcSc": s.bcSc, "bcSd": s.bcSd,
+            "bcXa": s.bcXa, "bcXb": s.bcXb, "bcXc": s.bcXc, "bcXd": s.bcXd,
+            "bcGa": s.bcGa, "bcGb": s.bcGb, "bcGc": s.bcGc, "bcGd": s.bcGd,
+            "bcHa": s.bcHa, "bcHb": s.bcHb, "bcHc": s.bcHc, "bcHd": s.bcHd}
+    tot = totals()
+
+    def ap(spec):
+        name, idx = spec
+        return bufs[name][idx if len(idx) > 1 else idx[0]]
+
+    def dst_id(d):
+        rid, pid, se = topo.addr(d)
+        return DstId(rid=rid, pnc=pid)
+
+    waited = set()
+    for op in prog(core):
+        if op[0] == "dma":
+            if op[4]:
+                g.dma_start(ap(op[1]), ap(op[2]), accum_op=AluOpType.add).then_inc(sems[op[3]], 16)
+            else:
+                g.dma_start(ap(op[1]), ap(op[2])).then_inc(sems[op[3]], 16)
+        elif op[0] == "wait":
+            g.wait_ge(sems[op[1]], tot[(core, op[1])])
+            waited.add(op[1])
+        else:
+            g.remote_dma_fused(
+                [RemoteDMATransfer(dst_ids=[dst_id(d) for d, spec in dsts], dma_engine_mask=mask, remote_sem=sems[sem],
+                                   srcs=[ap(x) for x in srcs], dsts=[ap(spec) for d, spec in dsts], alu_op=alu)
+                 for srcs, dsts, mask, sem, alu in op[1]],
+                local_sem=sems["snt"])
+    for name in SEMAPHORES:
+        if (core, name) in tot and name not in waited:
+            g.wait_ge(sems[name], tot[(core, name)])

@@ -1,26 +1,25 @@
 from concourse.bass import DstId, RemoteDMATransfer
 from concourse.mybir import AluOpType
 
-K = 2
-RS = 2
-SP3 = "ten"
+WID = (64, 64)
+K = len(WID)
+RS = 8
 ORDER = "AABB"
-FUSE = True
 
 ROOT = 11
-W = 128 // K
 SCRATCH = {
     "xs": ("sbuf", [128, 256], "float32"),
     "rl": ("sbuf", [128, 1024 if RS == 2 else 256], "float32"),
     "p0": ("dram", [128, 16], "float32"),
     "p1": ("dram", [128, 16], "float32"),
-    "bb": ("dram", [8 * K, 128, W], "float32"),
 }
+for rnd, wid in enumerate(WID):
+    SCRATCH["bb%d" % rnd] = ("dram", [8, 128, wid], "float32")
 SEMAPHORES = ["ld1", "y1a", "y1b", "snt", "rsA", "rs0", "rs1"] + [
     n + r for n in ("ld2", "y2", "bcS", "bcX", "bcG", "bcH") for r in "abcd"]
 
-CARRIER = (ROOT, ROOT, 10, 10, 14, 14, 15, 15)
-SPREADER = (8, 9, 10, 10, 14, 12, 15, 13)
+CARRIER = (ROOT, ROOT, ROOT, ROOT, 14, 14, 15, 15)
+SPREADER = (8, 9, 10, 12, 14, 13, 15, 13)
 ALL = (slice(None),)
 
 
@@ -33,13 +32,13 @@ def cols(a, n):
 
 
 def piece(t, j):
-    return ("bb", (8 * t + j,))
+    return ("bb%d" % t, (j,))
 
 
 def part(name, t):
     if name == "bb":
-        return (name, (slice(8 * t, 8 * t + 8),))
-    return (name, (slice(t * 128 // K, (t + 1) * 128 // K), slice(None)))
+        return ("bb%d" % t, ALL)
+    return (name, (slice(sum(WID[:t]), sum(WID[:t + 1])), slice(None)))
 
 
 def after(c, cores):
@@ -89,11 +88,10 @@ def rs_fold(c):
     return trs
 
 
-def spread(t, j, c, mask, dests=None, sem="bcG"):
-    if dests is None:
-        have = (ROOT, CARRIER[j], SPREADER[j])
-        dests = [d for d in range(8, 16) if d not in have]
-    return ([piece(t, j)], [(d, piece(t, j)) for d in after(c, dests)], mask, sem + "abcd"[t], 0)
+def spread(t, j, c, mask):
+    have = (ROOT, CARRIER[j], SPREADER[j])
+    dests = [d for d in range(8, 16) if d not in have]
+    return ([piece(t, j)], [(d, piece(t, j)) for d in after(c, dests)], mask, "bcG" + "abcd"[t], 0)
 
 
 def prog(c):
@@ -126,9 +124,10 @@ def prog(c):
             call(folds)
 
     if c == ROOT:
+        load_x1()
         for t in rounds:
             dma(part("bb", t), part("x2", t), "ld2" + "abcd"[t])
-        load_x1()
+        send_x1()
 
         def call_a(t):
             wait("ld2" + "abcd"[t])
@@ -136,28 +135,19 @@ def prog(c):
                    ("bcX" if CARRIER[j] == ROOT else "bcS") + "abcd"[t], 0) for j in range(8)])
 
         def call_b(t):
-            extra = [j for j in range(8) if SPREADER[j] != CARRIER[j]]
-            n = 4 if len(extra) <= 4 else 2
-            call([([piece(t, j)], [(SPREADER[j], piece(t, j))], eng(n * i, n), "bcS" + "abcd"[t], 0)
+            extra = [j for j in range(8) if CARRIER[j] == ROOT]
+            call([([piece(t, j)], [(SPREADER[j], piece(t, j))], eng(4 * i, 4), "bcS" + "abcd"[t], 0)
                   for i, j in enumerate(extra)])
-
-        def call_s(t):
-            if SP3 == "root":
-                call([spread(t, 3, c, 0xFFFF)])
 
         if ORDER == "ABAB":
             for t in rounds:
                 call_a(t)
                 call_b(t)
-                call_s(t)
         else:
             for t in rounds:
                 call_a(t)
             for t in rounds:
                 call_b(t)
-            for t in rounds:
-                call_s(t)
-        send_x1()
         fold_x1()
         dma(("y2", ALL), ("x2", ALL), "y2a")
         wait("rs0")
@@ -168,40 +158,30 @@ def prog(c):
 
     load_x1()
     send_x1()
-    if ch == 0:
-        fold_x1()
+    fold_x1()
     for t in rounds:
         if ch == 0:
             wait("bcX" + "abcd"[t])
             call([([piece(t, k)], [(d, piece(t, k)) for d in after(c, [d for d in range(8) if d != c])], 0xFFFF,
                    "bcG" + "abcd"[t], 0)])
         else:
-            wait("bcS" + "abcd"[t])
             carry = [j for j in range(8) if CARRIER[j] == c]
             own = [j for j in range(8) if SPREADER[j] == c]
             if carry:
-                over = [([piece(t, j)], [(j, piece(t, j))], eng(4 * i, 4), "bcX" + "abcd"[t], 0)
-                        for i, j in enumerate(carry)]
-                if FUSE:
-                    call(over + [spread(t, own[0], c, eng(8, 8))])
-                    own = own[1:]
-                else:
-                    call(over)
-            for j in own:
-                if j == 3 and SP3 == "root":
-                    continue
-                if j == 3 and SP3 == "two":
-                    call([spread(t, j, c, 0xFFFF, [12, 13], "bcH")])
-                else:
-                    call([spread(t, j, c, 0xFFFF)])
-    if SP3 == "two" and c in (12, 13):
-        for t in rounds:
-            wait("bcH" + "abcd"[t])
-            call([spread(t, 3, c, 0xFFFF, [8, 14] if c == 12 else [9, 15])])
+                wait("bcS" + "abcd"[t])
+                call([([piece(t, j)], [(j, piece(t, j))], eng(4 * i, 4), "bcX" + "abcd"[t], 0)
+                      for i, j in enumerate(carry)]
+                     + [([piece(t, j)], [(SPREADER[j], piece(t, j))], eng(8, 8), "bcH" + "abcd"[t], 0)
+                        for j in carry if SPREADER[j] != c])
+                call([spread(t, j, c, 0xFFFF) for j in own])
+            elif len(own) == 1:
+                wait("bcS" + "abcd"[t])
+                call([spread(t, own[0], c, 0xFFFF)])
+            else:
+                wait("bcH" + "abcd"[t])
+                call([spread(t, j, c, eng(8 * i, 8)) for i, j in enumerate(own)])
     wait("rs0")
     dma(("y1", ALL), ("p0", ALL), "y1a")
-    if ch == 1:
-        fold_x1()
     for t in rounds:
         wait("bcG" + "abcd"[t])
         dma(part("y2", t), part("bb", t), "y2" + "abcd"[t])
@@ -230,8 +210,14 @@ def totals():
 
 
 def rank_program(g, core, T, topo):
-    bufs = {"xs": T.xs, "rl": T.rl, "p0": T.p0, "p1": T.p1, "bb": T.bb,
+    bufs = {"xs": T.xs, "rl": T.rl, "p0": T.p0, "p1": T.p1, "bb0": T.bb0,
             "x1": T.x1, "x2": T.x2, "y1": T.y1, "y2": T.y2}
+    if K > 1:
+        bufs["bb1"] = T.bb1
+    if K > 2:
+        bufs["bb2"] = T.bb2
+    if K > 3:
+        bufs["bb3"] = T.bb3
     s = T.sem
     sems = {"ld1": s.ld1, "y1a": s.y1a, "y1b": s.y1b, "snt": s.snt, "rsA": s.rsA, "rs0": s.rs0, "rs1": s.rs1,
             "ld2a": s.ld2a, "ld2b": s.ld2b, "ld2c": s.ld2c, "ld2d": s.ld2d,

@@ -3,19 +3,18 @@ from concourse.mybir import AluOpType
 
 WID = (64, 64)
 K = len(WID)
-RS = 8
 ORDER = "AABB"
 
 ROOT = 11
 SCRATCH = {
     "xs": ("sbuf", [128, 256], "float32"),
-    "rl": ("sbuf", [128, 1024 if RS == 2 else 256], "float32"),
-    "p0": ("dram", [128, 16], "float32"),
-    "p1": ("dram", [128, 16], "float32"),
+    "rl": ("dram", [8, 128, 32], "float32"),
+    "p0": ("dram", [128, 32], "float32"),
+    "p1": ("dram", [128, 32], "float32"),
 }
 for rnd, wid in enumerate(WID):
     SCRATCH["bb%d" % rnd] = ("dram", [8, 128, wid], "float32")
-SEMAPHORES = ["ld1", "y1a", "y1b", "snt", "rsA", "rs0", "rs1"] + [
+SEMAPHORES = ["ld1", "ldo", "y1a", "y1b", "snt", "rsA", "rs0", "rs1"] + [
     n + r for n in ("ld2", "y2", "bcS", "bcX", "bcG", "bcH") for r in "abcd"]
 
 CARRIER = (ROOT, ROOT, ROOT, ROOT, 14, 14, 15, 15)
@@ -45,47 +44,26 @@ def after(c, cores):
     return sorted(cores, key=lambda d: (d - c) % 8)
 
 
-def groups(ch):
-    if RS == 2:
-        return [((3, 15)[ch], 0, list(range(4, 12))), ((7, 10)[ch], 128, [12, 13, 14, 15, 0, 1, 2, 3])]
-    out = []
-    for p in range(8):
-        red = 8 * ch + ((4, 0, 1, 5)[p % 4] if p // 4 == ch else (2, 3, 6, 7)[p % 4])
-        out.append((red, 32 * p, [2 * p, 2 * p + 1]))
-    return out
+def folder(ch, p):
+    return 8 * ch + ((4, 0, 1, 5)[p % 4] if p // 4 == ch else (2, 3, 6, 7)[p % 4])
 
 
-def rs_load(c):
-    if RS == 2:
-        return [(("xs", cols(0, 192)), ("x1", cols(64, 192))), (("xs", cols(192, 64)), ("x1", cols(0, 64)))]
-    return [(("xs", ALL), ("x1", ALL))]
+def my_pair(c):
+    return [p for p in range(8) if folder(c // 8, p) == c][0]
 
 
 def rs_send(c):
     ch, k = divmod(c, 8)
-    gs = [x for x in groups(ch) if x[0] != c]
-    n = 8 if RS == 2 else 2
-    return [([("xs", cols(a, 16 * len(rk)))], [(red, ("rl", cols(16 * len(rk) * k, 16 * len(rk))))], eng(n * i, n),
-             "rsA", 0) for i, (red, a, rk) in enumerate(gs)]
+    ps = [p for p in range(8) if folder(ch, p) != c]
+    return [([("xs", cols(32 * p, 32))], [(folder(ch, p), ("rl", (k,)))], eng(2 * i, 2), "rsA", 0)
+            for i, p in enumerate(ps)]
 
 
 def rs_fold(c):
-    ch, k = divmod(c, 8)
-    trs = []
-    for red, a, rk in groups(ch):
-        if red != c:
-            continue
-        w = 16 * len(rk)
-        far = [r for r in rk if r // 8 != ch]
-        near = [r for r in rk if r // 8 == ch]
-        nf = 8 // len(far) if far else 0
-        nn = (8 if far else 16) // len(near) if near else 0
-        for r in rk:
-            o = 16 * rk.index(r)
-            srcs = [("rl", cols(w * s + o, 16)) for s in range(8) if s != k] + [("xs", cols(a + o, 16))]
-            m = eng(nf * far.index(r), nf) if r in far else eng((8 if far else 0) + nn * near.index(r), nn)
-            trs.append((srcs, [(r, ("p%d" % ch, ALL))], m, "rs%d" % ch, 1))
-    return trs
+    ch = c // 8
+    p = my_pair(c)
+    return [([("rl", (s,)) for s in range(8)], [(r, ("p%d" % ch, ALL)) for r in (2 * p, 2 * p + 1)],
+             0xFFFF if p // 4 == ch else 0x00FF, "rs%d" % ch, 1)]
 
 
 def spread(t, j, c, mask):
@@ -98,7 +76,7 @@ def prog(c):
     ch, k = divmod(c, 8)
     ops = []
     rounds = range(K)
-    folds = rs_fold(c)
+    half = cols(16 * (c % 2), 16)
 
     def dma(out, in_, sem, add=False):
         ops.append(("dma", out, in_, sem, add))
@@ -111,17 +89,16 @@ def prog(c):
         ops.append(("rdma", trs))
 
     def load_x1():
-        for o, i in rs_load(c):
-            dma(o, i, "ld1")
+        dma(("xs", ALL), ("x1", ALL), "ld1")
+        dma(("rl", (k,)), ("x1", cols(32 * my_pair(c), 32)), "ldo")
 
     def send_x1():
         wait("ld1")
         call(rs_send(c))
 
     def fold_x1():
-        if folds:
-            wait("rsA")
-            call(folds)
+        wait("ldo", "rsA")
+        call(rs_fold(c))
 
     if c == ROOT:
         load_x1()
@@ -151,9 +128,9 @@ def prog(c):
         fold_x1()
         dma(("y2", ALL), ("x2", ALL), "y2a")
         wait("rs0")
-        dma(("y1", ALL), ("p0", ALL), "y1a")
+        dma(("y1", ALL), ("p0", half), "y1a")
         wait("rs1", "y1a")
-        dma(("y1", ALL), ("p1", ALL), "y1b", True)
+        dma(("y1", ALL), ("p1", half), "y1b", True)
         return ops
 
     load_x1()
@@ -181,12 +158,12 @@ def prog(c):
                 wait("bcH" + "abcd"[t])
                 call([spread(t, j, c, eng(8 * i, 8)) for i, j in enumerate(own)])
     wait("rs0")
-    dma(("y1", ALL), ("p0", ALL), "y1a")
+    dma(("y1", ALL), ("p0", half), "y1a")
     for t in rounds:
         wait("bcG" + "abcd"[t])
         dma(part("y2", t), part("bb", t), "y2" + "abcd"[t])
     wait("rs1", "y1a")
-    dma(("y1", ALL), ("p1", ALL), "y1b", True)
+    dma(("y1", ALL), ("p1", half), "y1b", True)
     return ops
 
 
@@ -219,7 +196,8 @@ def rank_program(g, core, T, topo):
     if K > 3:
         bufs["bb3"] = T.bb3
     s = T.sem
-    sems = {"ld1": s.ld1, "y1a": s.y1a, "y1b": s.y1b, "snt": s.snt, "rsA": s.rsA, "rs0": s.rs0, "rs1": s.rs1,
+    sems = {"ld1": s.ld1, "ldo": s.ldo, "y1a": s.y1a, "y1b": s.y1b, "snt": s.snt, "rsA": s.rsA, "rs0": s.rs0,
+            "rs1": s.rs1,
             "ld2a": s.ld2a, "ld2b": s.ld2b, "ld2c": s.ld2c, "ld2d": s.ld2d,
             "y2a": s.y2a, "y2b": s.y2b, "y2c": s.y2c, "y2d": s.y2d,
             "bcSa": s.bcSa, "bcSb": s.bcSb, "bcSc": s.bcSc, "bcSd": s.bcSd,

@@ -3,7 +3,6 @@ from concourse.mybir import AluOpType
 
 WID = (64, 64)
 K = len(WID)
-ORDER = "AABB"
 
 ROOT = 11
 SCRATCH = {
@@ -90,6 +89,8 @@ def prog(c):
 
     def load_x1():
         dma(("xs", ALL), ("x1", ALL), "ld1")
+
+    def load_own():
         dma(("rl", (k,)), ("x1", cols(32 * my_pair(c), 32)), "ldo")
 
     def send_x1():
@@ -104,36 +105,26 @@ def prog(c):
         load_x1()
         for t in rounds:
             dma(part("bb", t), part("x2", t), "ld2" + "abcd"[t])
+        load_own()
         send_x1()
-
-        def call_a(t):
+        for t in rounds:
             wait("ld2" + "abcd"[t])
             call([([piece(t, j)], [(j if CARRIER[j] == ROOT else CARRIER[j], piece(t, j))], eng(2 * j, 2),
                    ("bcX" if CARRIER[j] == ROOT else "bcS") + "abcd"[t], 0) for j in range(8)])
-
-        def call_b(t):
+        for t in rounds:
             extra = [j for j in range(8) if CARRIER[j] == ROOT]
             call([([piece(t, j)], [(SPREADER[j], piece(t, j))], eng(4 * i, 4), "bcS" + "abcd"[t], 0)
                   for i, j in enumerate(extra)])
-
-        if ORDER == "ABAB":
-            for t in rounds:
-                call_a(t)
-                call_b(t)
-        else:
-            for t in rounds:
-                call_a(t)
-            for t in rounds:
-                call_b(t)
         fold_x1()
-        dma(("y2", ALL), ("x2", ALL), "y2a")
         wait("rs0")
         dma(("y1", ALL), ("p0", half), "y1a")
+        dma(("y2", ALL), ("x2", ALL), "y2a")
         wait("rs1", "y1a")
         dma(("y1", ALL), ("p1", half), "y1b", True)
         return ops
 
     load_x1()
+    load_own()
     send_x1()
     fold_x1()
     for t in rounds:

@@ -102,15 +102,15 @@ def prog(c):
         call(rs_fold(c))
 
     if c == ROOT:
-        load_x1()
         for t in rounds:
             dma(part("bb", t), part("x2", t), "ld2" + "abcd"[t])
+        load_x1()
         load_own()
-        send_x1()
         for t in rounds:
             wait("ld2" + "abcd"[t])
             call([([piece(t, j)], [(j if CARRIER[j] == ROOT else CARRIER[j], piece(t, j))], eng(2 * j, 2),
                    ("bcX" if CARRIER[j] == ROOT else "bcS") + "abcd"[t], 0) for j in range(8)])
+        send_x1()
         for t in rounds:
             extra = [j for j in range(8) if CARRIER[j] == ROOT]
             call([([piece(t, j)], [(SPREADER[j], piece(t, j))], eng(4 * i, 4), "bcS" + "abcd"[t], 0)
@@ -126,7 +126,9 @@ def prog(c):
     load_x1()
     load_own()
     send_x1()
-    fold_x1()
+    late = c in (13, 14, 15)
+    if not late:
+        fold_x1()
     for t in rounds:
         if ch == 0:
             wait("bcX" + "abcd"[t])
@@ -148,6 +150,8 @@ def prog(c):
             else:
                 wait("bcH" + "abcd"[t])
                 call([spread(t, j, c, eng(8 * i, 8)) for i, j in enumerate(own)])
+    if late:
+        fold_x1()
     wait("rs0")
     dma(("y1", ALL), ("p0", half), "y1a")
     for t in rounds:

from concourse.bass import DstId, RemoteDMATransfer
from concourse.mybir import AluOpType

WID = (64, 64)
K = len(WID)

ROOT = 11
SCRATCH = {
    "xs": ("sbuf", [128, 256], "float32"),
    "rl": ("dram", [8, 128, 32], "float32"),
    "p0": ("dram", [128, 32], "float32"),
    "p1": ("dram", [128, 32], "float32"),
}
for rnd, wid in enumerate(WID):
    SCRATCH["bb%d" % rnd] = ("dram", [8, 128, wid], "float32")
SEMAPHORES = ["ld1", "ldo", "y1a", "y1b", "snt", "rsA", "rs0", "rs1"] + [
    n + r for n in ("ld2", "y2", "bcS", "bcX", "bcG", "bcH") for r in "abcd"]

CARRIER = (ROOT, ROOT, ROOT, ROOT, 14, 14, 15, 15)
SPREADER = (8, 9, 10, 12, 14, 13, 15, 13)
ALL = (slice(None),)


def eng(lo, n):
    return ((1 << n) - 1) << lo


def cols(a, n):
    return (slice(None), slice(a, a + n))


def piece(t, j):
    return ("bb%d" % t, (j,))


def part(name, t):
    if name == "bb":
        return ("bb%d" % t, ALL)
    return (name, (slice(sum(WID[:t]), sum(WID[:t + 1])), slice(None)))


def after(c, cores):
    return sorted(cores, key=lambda d: (d - c) % 8)


def folder(ch, p):
    return 8 * ch + ((4, 0, 1, 5)[p % 4] if p // 4 == ch else (2, 3, 6, 7)[p % 4])


def my_pair(c):
    return [p for p in range(8) if folder(c // 8, p) == c][0]


def rs_send(c):
    ch, k = divmod(c, 8)
    ps = [p for p in range(8) if folder(ch, p) != c]
    return [([("xs", cols(32 * p, 32))], [(folder(ch, p), ("rl", (k,)))], eng(2 * i, 2), "rsA", 0)
            for i, p in enumerate(ps)]


def rs_fold(c):
    ch = c // 8
    p = my_pair(c)
    return [([("rl", (s,)) for s in range(8)], [(r, ("p%d" % ch, ALL)) for r in (2 * p, 2 * p + 1)],
             0xFFFF if p // 4 == ch else 0x00FF, "rs%d" % ch, 1)]


def spread(t, j, c, mask):
    have = (ROOT, CARRIER[j], SPREADER[j])
    dests = [d for d in range(8, 16) if d not in have]
    return ([piece(t, j)], [(d, piece(t, j)) for d in after(c, dests)], mask, "bcG" + "abcd"[t], 0)


def prog(c):
    ch, k = divmod(c, 8)
    ops = []
    rounds = range(K)
    half = cols(16 * (c % 2), 16)

    def dma(out, in_, sem, add=False):
        ops.append(("dma", out, in_, sem, add))

    def wait(*sems):
        for s in sems:
            ops.append(("wait", s))

    def call(trs):
        ops.append(("rdma", trs))

    def load_x1():
        dma(("xs", ALL), ("x1", ALL), "ld1")

    def load_own():
        dma(("rl", (k,)), ("x1", cols(32 * my_pair(c), 32)), "ldo")

    def send_x1():
        wait("ld1")
        call(rs_send(c))

    def fold_x1():
        wait("ldo", "rsA")
        call(rs_fold(c))

    if c == ROOT:
        for t in rounds:
            dma(part("bb", t), part("x2", t), "ld2" + "abcd"[t])
        load_x1()
        load_own()
        for t in rounds:
            wait("ld2" + "abcd"[t])
            call([([piece(t, j)], [(j if CARRIER[j] == ROOT else CARRIER[j], piece(t, j))], eng(2 * j, 2),
                   ("bcX" if CARRIER[j] == ROOT else "bcS") + "abcd"[t], 0) for j in range(8)])
        send_x1()
        for t in rounds:
            extra = [j for j in range(8) if CARRIER[j] == ROOT]
            call([([piece(t, j)], [(SPREADER[j], piece(t, j))], eng(4 * i, 4), "bcS" + "abcd"[t], 0)
                  for i, j in enumerate(extra)])
        fold_x1()
        wait("rs0")
        dma(("y1", ALL), ("p0", half), "y1a")
        dma(("y2", ALL), ("x2", ALL), "y2a")
        wait("rs1", "y1a")
        dma(("y1", ALL), ("p1", half), "y1b", True)
        return ops

    load_x1()
    load_own()
    send_x1()
    late = c in (13, 14, 15)
    if not late:
        fold_x1()
    for t in rounds:
        if ch == 0:
            wait("bcX" + "abcd"[t])
            call([([piece(t, k)], [(d, piece(t, k)) for d in after(c, [d for d in range(8) if d != c])], 0xFFFF,
                   "bcG" + "abcd"[t], 0)])
        else:
            carry = [j for j in range(8) if CARRIER[j] == c]
            own = [j for j in range(8) if SPREADER[j] == c]
            if carry:
                wait("bcS" + "abcd"[t])
                call([([piece(t, j)], [(j, piece(t, j))], eng(4 * i, 4), "bcX" + "abcd"[t], 0)
                      for i, j in enumerate(carry)]
                     + [([piece(t, j)], [(SPREADER[j], piece(t, j))], eng(8, 8), "bcH" + "abcd"[t], 0)
                        for j in carry if SPREADER[j] != c])
                call([spread(t, j, c, 0xFFFF) for j in own])
            elif len(own) == 1:
                wait("bcS" + "abcd"[t])
                call([spread(t, own[0], c, 0xFFFF)])
            else:
                wait("bcH" + "abcd"[t])
                call([spread(t, j, c, eng(8 * i, 8)) for i, j in enumerate(own)])
    if late:
        fold_x1()
    wait("rs0")
    dma(("y1", ALL), ("p0", half), "y1a")
    for t in rounds:
        wait("bcG" + "abcd"[t])
        dma(part("y2", t), part("bb", t), "y2" + "abcd"[t])
    wait("rs1", "y1a")
    dma(("y1", ALL), ("p1", half), "y1b", True)
    return ops


def totals():
    tot = {}

    def add(c, s, n):
        tot[(c, s)] = tot.get((c, s), 0) + n

    for c in range(16):
        for op in prog(c):
            if op[0] == "dma":
                add(c, op[3], 16)
            elif op[0] == "rdma":
                for srcs, dsts, mask, sem, alu in op[1]:
                    n = bin(mask).count("1")
                    add(c, "snt", n)
                    for d, spec in dsts:
                        add(d, sem, n)
    return tot


def rank_program(g, core, T, topo):
    bufs = {"xs": T.xs, "rl": T.rl, "p0": T.p0, "p1": T.p1, "bb0": T.bb0,
            "x1": T.x1, "x2": T.x2, "y1": T.y1, "y2": T.y2}
    if K > 1:
        bufs["bb1"] = T.bb1
    if K > 2:
        bufs["bb2"] = T.bb2
    if K > 3:
        bufs["bb3"] = T.bb3
    s = T.sem
    sems = {"ld1": s.ld1, "ldo": s.ldo, "y1a": s.y1a, "y1b": s.y1b, "snt": s.snt, "rsA": s.rsA, "rs0": s.rs0,
            "rs1": s.rs1,
            "ld2a": s.ld2a, "ld2b": s.ld2b, "ld2c": s.ld2c, "ld2d": s.ld2d,
            "y2a": s.y2a, "y2b": s.y2b, "y2c": s.y2c, "y2d": s.y2d,
            "bcSa": s.bcSa, "bcSb": s.bcSb, "bcSc": s.bcSc, "bcSd": s.bcSd,
            "bcXa": s.bcXa, "bcXb": s.bcXb, "bcXc": s.bcXc, "bcXd": s.bcXd,
            "bcGa": s.bcGa, "bcGb": s.bcGb, "bcGc": s.bcGc, "bcGd": s.bcGd,
            "bcHa": s.bcHa, "bcHb": s.bcHb, "bcHc": s.bcHc, "bcHd": s.bcHd}
    tot = totals()

    def ap(spec):
        name, idx = spec
        return bufs[name][idx if len(idx) > 1 else idx[0]]

    def dst_id(d):
        rid, pid, se = topo.addr(d)
        return DstId(rid=rid, pnc=pid)

    waited = set()
    for op in prog(core):
        if op[0] == "dma":
            if op[4]:
                g.dma_start(ap(op[1]), ap(op[2]), accum_op=AluOpType.add).then_inc(sems[op[3]], 16)
            else:
                g.dma_start(ap(op[1]), ap(op[2])).then_inc(sems[op[3]], 16)
        elif op[0] == "wait":
            g.wait_ge(sems[op[1]], tot[(core, op[1])])
            waited.add(op[1])
        else:
            g.remote_dma_fused(
                [RemoteDMATransfer(dst_ids=[dst_id(d) for d, spec in dsts], dma_engine_mask=mask, remote_sem=sems[sem],
                                   srcs=[ap(x) for x in srcs], dsts=[ap(spec) for d, spec in dsts], alu_op=alu)
                 for srcs, dsts, mask, sem, alu in op[1]],
                local_sem=sems["snt"])
    for name in SEMAPHORES:
        if (core, name) in tot and name not in waited:
            g.wait_ge(sems[name], tot[(core, name)])
